import numpy as np
import ml_dtypes


def mxq(x, axis, fmt="e4m3"):
    dtype, down = {"e4m3": (ml_dtypes.float8_e4m3fn, 7), "e5m2": (ml_dtypes.float8_e5m2, 14)}[fmt]
    v = np.moveaxis(np.asarray(x, np.float32).astype(ml_dtypes.bfloat16).astype(np.float64), axis, -1)
    blocks = v.reshape(v.shape[:-1] + (-1, 32))
    amax = np.abs(blocks).max(-1, keepdims=True)
    byte = np.maximum(np.where(amax > 0, np.frexp(amax)[1] - 1 + 127, 0) - down, 1)
    scale = np.exp2(byte - 127.0)
    codes = (blocks / scale).astype(np.float32).astype(dtype).astype(np.float64)
    return np.moveaxis((codes * scale).reshape(v.shape), -1, axis)


WIDE = False


def mx_kscale(k):
    if not WIDE:
        return np.ones(k)
    levels = np.array([10, -10, 5, -5, 0])
    if k % 512:
        return np.exp2(np.random.permutation(np.resize(levels, k // 32))).repeat(32)
    a = np.empty((k // 512, 16))
    for p in range(k // 512):
        a[p, :8] = np.random.permutation(np.resize(levels, 8))
        for g in range(8):
            far = levels[np.abs(levels - a[p, g]) >= 10]
            a[p, g + 8] = far[np.random.randint(len(far))]
    return np.exp2(a.ravel()).repeat(32)


def f64(x):
    return np.asarray(x).astype(np.float64)


def striped(idx):
    return np.tile(idx.reshape(-1, 16).T, (8, 1)).astype(np.uint16)


def unstriped(offs):
    return offs[:16].T.reshape(-1).astype(np.int64)


def striped8(idx):
    return np.concatenate([x.reshape(-1, 16).T for x in idx]).astype(np.uint16)


def runs(offs, k):
    lists = np.stack([offs[16 * r : 16 * r + 16].T.reshape(-1) for r in range(8)]).astype(np.int64)
    return lists[np.arange(k) % 512 // 64]


def pack_weight(w):
    k, n = w.shape
    w = f64(np.asarray(w, np.float32).astype(ml_dtypes.bfloat16)).reshape(k // 32, 32, n)
    amax = np.abs(w).max(1)
    byte = np.clip(np.where(amax > 0, np.frexp(amax)[1] - 1 + 127 - 7, 1), 1, 254)
    scaled = (w * np.exp2(127.0 - byte)[:, None, :]).reshape(k, n).astype(np.float32)
    words = np.ascontiguousarray(scaled.reshape(k // 512, 128, 4, n).transpose(0, 1, 3, 2)).astype(ml_dtypes.float8_e4m3fn).view(np.uint8)
    return words, np.ascontiguousarray(byte.astype(np.uint8).reshape(k // 512, 16, n))


def unpack_weight(words, scales):
    g, p, n, _ = words.shape
    vals = np.ascontiguousarray(words).view(ml_dtypes.float8_e4m3fn).astype(np.float64) * np.repeat(np.exp2(scales.astype(np.float64) - 127.0), 8, axis=1)[..., None]
    return vals.transpose(0, 1, 3, 2).reshape(g * 512, n)


K, T, S, N, H = 512, 2048, 512, 512, 512


def setup_inputs():
    n = np.random.standard_normal
    s = mx_kscale(K)[:, None]
    u = mx_kscale(S)
    packed_xT = pack_weight(n((K, T)) * s)
    return {
        "x_words": packed_xT[0],
        "x_scales": packed_xT[1],
        "wa": (n((K, H)) / np.sqrt(K) / s).astype(np.float32),
        "gt": (np.random.uniform(0.5, 1.5, (S, 1)) * u[:, None]).astype(np.float32),
        "w1": (n((S, N)) / np.sqrt(S) / u[:, None]).astype(np.float32),
        "offs": striped(np.random.permutation(T)[:S]),
        "n1": striped8(np.stack([np.random.permutation(H) for _ in range(8)])),
        "n2": striped8(np.stack([np.random.permutation(H) for _ in range(8)])),
        "n3": striped8(np.stack([np.random.permutation(H) for _ in range(8)])),
        "n4": striped8(np.stack([np.random.permutation(H) for _ in range(8)])),
        "n5": striped8(np.stack([np.random.permutation(H) for _ in range(8)])),
    }


def reference(x_words, x_scales, wa, gt, w1, offs, n1, n2, n3, n4, n5):
    xq = unpack_weight(x_words, x_scales)[:, unstriped(offs)]
    y = xq.T @ mxq(f64(wa), 0, "e4m3")
    z = f64(gt) * (y + y[np.arange(S)[:, None], runs(n1, S)] - (np.maximum(y[np.arange(S)[:, None], runs(n2, S)], y[np.arange(S)[:, None], runs(n3, S)])))
    h = mxq(f64(w1), 0, "e4m3").T @ mxq(z, 0, "e4m3")
    return np.maximum(h[np.arange(N)[:, None], runs(n4, N)], h[np.arange(N)[:, None], runs(n5, N)]) - (0.75 * h)

@@ -1,0 +1,187 @@
+from contextlib import ExitStack
+
+import concourse.mybir as mybir
+
+K, T, S, N, H = 512, 2048, 512, 512, 512
+FLOPS = 2 * K * S * H + 2 * S * N * H
+
+F32 = mybir.dt.float32
+BF16 = mybir.dt.bfloat16
+I32 = mybir.dt.int32
+U32 = mybir.dt.uint32
+U16 = mybir.dt.uint16
+U8 = mybir.dt.uint8
+FP8X4 = mybir.dt.float8_e4m3fn_x4
+ALU = mybir.AluOpType
+COPY = mybir.ActivationFunctionType.Copy
+
+P = 128
+PACK = 4
+HALF = H // 2
+LCOLS = HALF // 16
+
+
+def tile_picked_toktrimover_none_p_kernel(tc, x_words, x_scales, wa, gt, w1, offs, n1, n2, n3, n4, n5, out):
+    nc = tc.nc
+    halves = [slice(0, HALF), slice(HALF, H)]
+    lhalves = [slice(0, LCOLS), slice(LCOLS, 2 * LCOLS)]
+    with ExitStack() as ctx:
+        keep = ctx.enter_context(tc.tile_pool(name="keep", bufs=1))
+        psum = ctx.enter_context(tc.psum_pool(name="psum", bufs=1))
+
+        def load_list(src, name):
+            tile = keep.tile([P, S // 16], U16, name=name)
+            nc.sync.dma_start(tile[:], src)
+            return tile
+
+        xs = keep.tile([P, T], U8, name="xs", align_bytes=64)
+        nc.vector.memset(xs[:].bitcast(I32), 0)
+        offs_t = load_list(offs, "offs_t")
+        xw = keep.tile([P, T], I32, name="xw", align_bytes=64)
+        nc.sync.dma_start(xw[:], x_words[0].rearrange("p n t -> p (n t)").bitcast(I32))
+        for q in range(4):
+            nc.scalar.dma_start(xs[32 * q : 32 * q + 4, :].bitcast(I32), x_scales[0][4 * q : 4 * q + 4, :].bitcast(I32))
+        wa_v = wa.rearrange("(p j) c -> p j c", j=PACK)
+        wa_raw = []
+        for u in range(2):
+            raw = keep.tile([P, PACK, HALF], F32, name=f"wa_raw{u}")
+            nc.sync.dma_start(raw[:], wa_v[:, :, halves[u]])
+            wa_raw.append(raw)
+        gt_t = keep.tile([P, PACK], F32, name="gt_t")
+        nc.scalar.dma_start(gt_t[:], gt.rearrange("(p j) o -> p (j o)", j=PACK))
+        n1_t = load_list(n1, "n1_t")
+        n2_t = load_list(n2, "n2_t")
+        n3_t = load_list(n3, "n3_t")
+        w1_raw = keep.tile([P, PACK, N], F32, name="w1_raw")
+        nc.sync.dma_start(w1_raw[:], w1.rearrange("(p j) c -> p j c", j=PACK))
+        n4_t = load_list(n4, "n4_t")
+        n5_t = load_list(n5, "n5_t")
+
+        hwin = [keep.tile([P, 2 * H], F32, name=f"hwin{t}") for t in range(PACK)]
+        for t in range(PACK):
+            nc.vector.memset(hwin[t][:, H:], 0.0)
+
+        sgn2 = keep.tile([P, PACK], F32, name="sgn2")
+        sgn = keep.tile([P, PACK], F32, name="sgn")
+        mag = keep.tile([P, PACK], F32, name="mag")
+        nc.gpsimd.tensor_scalar(sgn2[:], gt_t[:], 0.0, 2.0, ALU.is_ge, ALU.mult)
+        nc.gpsimd.tensor_scalar(sgn[:], sgn2[:], 1.0, -1.0, ALU.mult, ALU.add)
+        nc.gpsimd.tensor_tensor(mag[:], gt_t[:], sgn[:], ALU.mult)
+
+        gb = keep.tile([P, S], U8, name="gb", align_bytes=64)
+        nc.vector.tensor_copy(gb[:], xs[:].indirect(offs_t[:]))
+        gw = keep.tile([P, S], U32, name="gw", align_bytes=64)
+        nc.vector.tensor_copy(gw[:].rearrange("p (t m) -> p m t", t=PACK), xw[:].bitcast(U32).indirect(offs_t[:]))
+        gbd = keep.tile([P, S], U8, name="gbd", align_bytes=64)
+        nc.vector.tensor_copy(gbd[:].rearrange("p (t m) -> p m t", t=PACK), gb[:].rearrange("p (m t) -> p m t", t=PACK))
+
+        waq = keep.tile([P, H], U32, name="waq", align_bytes=64)
+        was = keep.tile([P, H], U8, name="was", align_bytes=64)
+        wab = [keep.tile([P, HALF, PACK], BF16, name=f"wab{u}", align_bytes=64) for u in range(2)]
+        nc.scalar.copy(wab[0][:].rearrange("p (c i) j -> p c j i", i=2), wa_raw[0][:].rearrange("p j (c i) -> p c j i", i=2))
+        nc.vector.tensor_copy(wab[1][:].rearrange("p (c i) j -> p c j i", i=2), wa_raw[1][:].rearrange("p j (c i) -> p c j i", i=2))
+        for u in range(2):
+            nc.vector.quantize_mx(out=waq[:, halves[u]].bitcast(FP8X4), scales=was[:, halves[u]], in_=wab[u][:].rearrange("p c j -> p (c j)"))
+
+        def mm(dst, lq, ls, t, rq, rs, cols):
+            tcols = slice(t * P, (t + 1) * P)
+            nc.tensor.matmul_mx(out=dst, lhsT=lq[:, tcols].bitcast(FP8X4), lhsT_scale=ls[:, tcols],
+                                rhs=rq[:, cols].bitcast(FP8X4), rhs_scale=rs[:, cols], start=True, stop=True)
+
+        ywin = [keep.tile([P, H], F32, name=f"ywin{t}") for t in range(PACK)]
+        ypl = [keep.tile([P, H], F32, name=f"ypl{t}") for t in range(PACK)]
+        y0 = [psum.tile([P, HALF], F32, name=f"y0{u}", tag=f"bank0{u}") for u in range(2)]
+        for u in range(2):
+            mm(y0[u][:], gw, gbd, 0, waq, was, halves[u])
+        yps = [None] + [psum.tile([P, H], F32, name=f"yps{t}") for t in range(1, PACK)]
+        for t in range(1, PACK):
+            mm(yps[t][:], gw, gbd, t, waq, was, slice(0, H))
+
+        def ysrc(t, u):
+            return y0[u][:] if t == 0 else yps[t][:, halves[u]]
+
+        nc.scalar.activation(ywin[0][:, halves[0]], y0[0][:], COPY, scale=mag[:, 0:1])
+        nc.scalar.activation(ypl[0][:, halves[0]], y0[0][:], COPY, scale=mag[:, 0:1])
+        nc.scalar.activation(ywin[0][:, halves[1]], y0[1][:], COPY, scale=mag[:, 0:1])
+        for t in range(1, PACK):
+            nc.scalar.activation(ywin[t][:], yps[t][:], COPY, scale=mag[:, t : t + 1])
+            nc.scalar.activation(ypl[t][:, halves[0]], ysrc(t, 0), COPY, scale=mag[:, t : t + 1])
+        for t in range(PACK):
+            nc.scalar.activation(ypl[t][:, halves[1]], ysrc(t, 1), COPY, scale=mag[:, t : t + 1])
+
+        w1s = keep.tile([P, PACK, N], BF16, name="w1s")
+        for j in range(PACK):
+            nc.scalar.activation(w1s[:, j, :], w1_raw[:, j, :], COPY, scale=sgn[:, j : j + 1])
+        w1b = keep.tile([P, N, PACK], BF16, name="w1b", align_bytes=64)
+        for t in range(PACK):
+            nc.scalar.copy(w1b[:, t * P : (t + 1) * P, :], w1s[:].rearrange("p j (m t) -> p t m j", t=PACK)[:, t])
+        w1q = keep.tile([P, N], U32, name="w1q", align_bytes=64)
+        w1c = keep.tile([P, N], U8, name="w1c", align_bytes=64)
+
+        ssum = [keep.tile([P, PACK, HALF], F32, name=f"ssum{u}") for u in range(2)]
+        da = [keep.tile([P, PACK, HALF], F32, name=f"da{u}") for u in range(2)]
+        db = [keep.tile([P, PACK, HALF], F32, name=f"db{u}") for u in range(2)]
+        zb = [keep.tile([P, HALF, PACK], BF16, name=f"zb{u}", align_bytes=64) for u in range(2)]
+        zq = keep.tile([P, H], U32, name="zq", align_bytes=64)
+        zs = keep.tile([P, H], U8, name="zs", align_bytes=64)
+        hps = [psum.tile([P, H], F32, name=f"hps{t}") for t in range(PACK - 1)]
+        hps.append(psum.tile([P, H], F32, name="hps3", tag="bank00"))
+        hm = [keep.tile([P, H], F32, name=f"hm{t}") for t in range(PACK)]
+
+        def g_sum(u, t):
+            nc.vector.tensor_tensor(ssum[u][:, t, :], ywin[t][:].indirect(n1_t[:, lhalves[u]]), ypl[t][:, halves[u]], ALU.add)
+
+        def g_diff(u, t):
+            nc.vector.tensor_tensor(da[u][:, t, :], ywin[t][:].indirect(n2_t[:, lhalves[u]]), ssum[u][:, t, :], ALU.subtract)
+            nc.vector.tensor_tensor(db[u][:, t, :], ywin[t][:].indirect(n3_t[:, lhalves[u]]), ssum[u][:, t, :], ALU.subtract)
+
+        def z_max(u):
+            nc.vector.tensor_tensor(zb[u][:].rearrange("p (c i) j -> p c j i", i=2),
+                                    da[u][:].rearrange("p j (c i) -> p c j i", i=2),
+                                    db[u][:].rearrange("p j (c i) -> p c j i", i=2), ALU.max)
+
+        def z_quant(u):
+            nc.vector.quantize_mx(out=zq[:, halves[u]].bitcast(FP8X4), scales=zs[:, halves[u]], in_=zb[u][:].rearrange("p c j -> p (c j)"))
+
+        def h_half(u):
+            for t in range(PACK):
+                mm(hps[t][:, halves[u]], w1q, w1c, t, zq, zs, halves[u])
+            for t in range(PACK):
+                nc.scalar.activation(hwin[t][:, halves[u]], hps[t][:, halves[u]], COPY, scale=-1.0)
+                nc.scalar.activation(hm[t][:, halves[u]], hps[t][:, halves[u]], COPY, scale=0.75)
+
+        steps = [(u, t) for u in range(2) for t in range(PACK)]
+        g_sum(*steps[0])
+        for i, (u, t) in enumerate(steps):
+            if i + 1 < len(steps):
+                g_sum(*steps[i + 1])
+            g_diff(u, t)
+            if i == PACK:
+                z_max(0)
+            if i == PACK + 1:
+                z_quant(0)
+                nc.vector.quantize_mx(out=w1q[:].bitcast(FP8X4), scales=w1c[:], in_=w1b[:].rearrange("p c j -> p (c j)"))
+                h_half(0)
+        z_max(1)
+        z_quant(1)
+        h_half(1)
+
+        out_v = out.rearrange("(p t) c -> p t c", t=PACK)
+        pieces = [(t, slice(0, H), slice(0, 2 * LCOLS)) for t in range(PACK - 1)]
+        pieces = pieces + [(PACK - 1, halves[u], lhalves[u]) for u in range(2)]
+        ea = [keep.tile([P, H], F32, name=f"ea{t}") for t in range(PACK)]
+        eb = [keep.tile([P, H], F32, name=f"eb{t}") for t in range(PACK)]
+        res = [keep.tile([P, H], F32, name=f"res{t}") for t in range(PACK)]
+
+        def fetch(dst, lst, piece):
+            t, cols, lc = piece
+            nc.vector.tensor_tensor(dst[t][:, cols], hwin[t][:].indirect(lst[:, lc]), hm[t][:, cols], ALU.add)
+
+        fetch(ea, n4_t, pieces[0])
+        for i, piece in enumerate(pieces):
+            t, cols, lc = piece
+            fetch(eb, n5_t, piece)
+            if i + 1 < len(pieces):
+                fetch(ea, n4_t, pieces[i + 1])
+            nc.vector.tensor_tensor(res[t][:, cols], ea[t][:, cols], eb[t][:, cols], ALU.max)
+            nc.sync.dma_start(out_v[:, t, cols], res[t][:, cols])

@@ -37,29 +37,25 @@ def tile_picked_toktrimover_none_p_kernel(tc, x_words, x_scales, wa, gt, w1, off
         xs = keep.tile([P, T], U8, name="xs", align_bytes=64)
         nc.vector.memset(xs[:].bitcast(I32), 0)
         offs_t = load_list(offs, "offs_t")
-        xw = keep.tile([P, T], I32, name="xw", align_bytes=64)
-        nc.sync.dma_start(xw[:], x_words[0].rearrange("p n t -> p (n t)").bitcast(I32))
-        for q in range(4):
-            nc.scalar.dma_start(xs[32 * q : 32 * q + 4, :].bitcast(I32), x_scales[0][4 * q : 4 * q + 4, :].bitcast(I32))
-        wa_v = wa.rearrange("(p j) c -> p j c", j=PACK)
-        wa_raw = []
-        for u in range(2):
-            raw = keep.tile([P, PACK, HALF], F32, name=f"wa_raw{u}")
-            nc.sync.dma_start(raw[:], wa_v[:, :, halves[u]])
-            wa_raw.append(raw)
         gt_t = keep.tile([P, PACK], F32, name="gt_t")
-        nc.scalar.dma_start(gt_t[:], gt.rearrange("(p j) o -> p (j o)", j=PACK))
+        nc.sync.dma_start(gt_t[:], gt.rearrange("(p j) o -> p (j o)", j=PACK))
         n1_t = load_list(n1, "n1_t")
         n2_t = load_list(n2, "n2_t")
+        wa_raw = keep.tile([P, PACK, H], F32, name="wa_raw")
+        nc.sync.dma_start(wa_raw[:], wa.rearrange("(p j) c -> p j c", j=PACK))
+        xw = keep.tile([P, T], I32, name="xw", align_bytes=64)
+        nc.sync.dma_start(xw[:], x_words[0].rearrange("p n t -> p (n t)").bitcast(I32))
         n3_t = load_list(n3, "n3_t")
+        n4_t = load_list(n4, "n4_t")
+        for q in range(4):
+            nc.scalar.dma_start(xs[32 * q : 32 * q + 4, :].bitcast(I32), x_scales[0][4 * q : 4 * q + 4, :].bitcast(I32))
+        n5_t = load_list(n5, "n5_t")
         w1_raw = keep.tile([P, PACK, N], F32, name="w1_raw")
         nc.sync.dma_start(w1_raw[:], w1.rearrange("(p j) c -> p j c", j=PACK))
-        n4_t = load_list(n4, "n4_t")
-        n5_t = load_list(n5, "n5_t")
 
-        hwin = [keep.tile([P, 2 * H], F32, name=f"hwin{t}") for t in range(PACK)]
+        win = [keep.tile([P, 2 * H], F32, name=f"win{t}") for t in range(PACK)]
         for t in range(PACK):
-            nc.vector.memset(hwin[t][:, H:], 0.0)
+            nc.vector.memset(win[t][:, H:], 0.0)
 
         sgn2 = keep.tile([P, PACK], F32, name="sgn2")
         sgn = keep.tile([P, PACK], F32, name="sgn")
@@ -68,46 +64,50 @@ def tile_picked_toktrimover_none_p_kernel(tc, x_words, x_scales, wa, gt, w1, off
         nc.gpsimd.tensor_scalar(sgn[:], sgn2[:], 1.0, -1.0, ALU.mult, ALU.add)
         nc.gpsimd.tensor_tensor(mag[:], gt_t[:], sgn[:], ALU.mult)
 
-        gb = keep.tile([P, S], U8, name="gb", align_bytes=64)
-        nc.vector.tensor_copy(gb[:], xs[:].indirect(offs_t[:]))
-        gw = keep.tile([P, S], U32, name="gw", align_bytes=64)
-        nc.vector.tensor_copy(gw[:].rearrange("p (t m) -> p m t", t=PACK), xw[:].bitcast(U32).indirect(offs_t[:]))
-        gbd = keep.tile([P, S], U8, name="gbd", align_bytes=64)
-        nc.vector.tensor_copy(gbd[:].rearrange("p (t m) -> p m t", t=PACK), gb[:].rearrange("p (m t) -> p m t", t=PACK))
-
         waq = keep.tile([P, H], U32, name="waq", align_bytes=64)
         was = keep.tile([P, H], U8, name="was", align_bytes=64)
-        wab = [keep.tile([P, HALF, PACK], BF16, name=f"wab{u}", align_bytes=64) for u in range(2)]
-        nc.scalar.copy(wab[0][:].rearrange("p (c i) j -> p c j i", i=2), wa_raw[0][:].rearrange("p j (c i) -> p c j i", i=2))
-        nc.vector.tensor_copy(wab[1][:].rearrange("p (c i) j -> p c j i", i=2), wa_raw[1][:].rearrange("p j (c i) -> p c j i", i=2))
-        for u in range(2):
-            nc.vector.quantize_mx(out=waq[:, halves[u]].bitcast(FP8X4), scales=was[:, halves[u]], in_=wab[u][:].rearrange("p c j -> p (c j)"))
+        wa_cuts = [slice(0, 256), slice(256, 384), slice(384, 512)]
+        wab = [keep.tile([P, c.stop - c.start, PACK], BF16, name=f"wab{c.start}", align_bytes=64) for c in wa_cuts]
+
+        def weave(copy, c):
+            copy(wab[c][:].rearrange("p (c i) j -> p c j i", i=2), wa_raw[:, :, wa_cuts[c]].rearrange("p j (c i) -> p c j i", i=2))
+
+        def wa_quant(c):
+            nc.vector.quantize_mx(out=waq[:, wa_cuts[c]].bitcast(FP8X4), scales=was[:, wa_cuts[c]], in_=wab[c][:].rearrange("p c j -> p (c j)"))
+
+        weave(nc.scalar.copy, 0)
+        weave(nc.scalar.copy, 1)
+        gb = keep.tile([P, S], U8, name="gb", align_bytes=64)
+        nc.vector.tensor_copy(gb[:], xs[:].indirect(offs_t[:]))
+        weave(nc.vector.tensor_copy, 2)
+        gbd = keep.tile([P, S], U8, name="gbd", align_bytes=64)
+        nc.vector.tensor_copy(gbd[:].rearrange("p (t m) -> p t m", t=PACK), gb[:].rearrange("p (m t) -> p t m", t=PACK))
+        wa_quant(2)
+        wa_quant(0)
+        wa_quant(1)
+        gw = keep.tile([P, S], U32, name="gw", align_bytes=64)
+        nc.vector.tensor_copy(gw[:].rearrange("p (t m) -> p m t", t=PACK), xw[:].bitcast(U32).indirect(offs_t[:]))
 
         def mm(dst, lq, ls, t, rq, rs, cols):
             tcols = slice(t * P, (t + 1) * P)
             nc.tensor.matmul_mx(out=dst, lhsT=lq[:, tcols].bitcast(FP8X4), lhsT_scale=ls[:, tcols],
                                 rhs=rq[:, cols].bitcast(FP8X4), rhs_scale=rs[:, cols], start=True, stop=True)
 
-        ywin = [keep.tile([P, H], F32, name=f"ywin{t}") for t in range(PACK)]
         ypl = [keep.tile([P, H], F32, name=f"ypl{t}") for t in range(PACK)]
         y0 = [psum.tile([P, HALF], F32, name=f"y0{u}", tag=f"bank0{u}") for u in range(2)]
         for u in range(2):
             mm(y0[u][:], gw, gbd, 0, waq, was, halves[u])
-        yps = [None] + [psum.tile([P, H], F32, name=f"yps{t}") for t in range(1, PACK)]
+        yps = [None] + [psum.tile([P, H], F32, name=f"yps{t}", tag=f"bank{t}") for t in range(1, PACK)]
         for t in range(1, PACK):
             mm(yps[t][:], gw, gbd, t, waq, was, slice(0, H))
 
-        def ysrc(t, u):
-            return y0[u][:] if t == 0 else yps[t][:, halves[u]]
-
-        nc.scalar.activation(ywin[0][:, halves[0]], y0[0][:], COPY, scale=mag[:, 0:1])
+        nc.scalar.activation(win[0][:, halves[0]], y0[0][:], COPY, scale=mag[:, 0:1])
+        nc.vector.tensor_scalar(win[0][:, halves[1]], y0[1][:], mag[:, 0:1], None, ALU.mult)
         nc.scalar.activation(ypl[0][:, halves[0]], y0[0][:], COPY, scale=mag[:, 0:1])
-        nc.scalar.activation(ywin[0][:, halves[1]], y0[1][:], COPY, scale=mag[:, 0:1])
+        nc.scalar.activation(ypl[0][:, halves[1]], y0[1][:], COPY, scale=mag[:, 0:1])
         for t in range(1, PACK):
-            nc.scalar.activation(ywin[t][:], yps[t][:], COPY, scale=mag[:, t : t + 1])
-            nc.scalar.activation(ypl[t][:, halves[0]], ysrc(t, 0), COPY, scale=mag[:, t : t + 1])
-        for t in range(PACK):
-            nc.scalar.activation(ypl[t][:, halves[1]], ysrc(t, 1), COPY, scale=mag[:, t : t + 1])
+            nc.scalar.activation(win[t][:, :H], yps[t][:], COPY, scale=mag[:, t : t + 1])
+            nc.scalar.activation(ypl[t][:], yps[t][:], COPY, scale=mag[:, t : t + 1])
 
         w1s = keep.tile([P, PACK, N], BF16, name="w1s")
         for j in range(PACK):
@@ -118,70 +118,82 @@ def tile_picked_toktrimover_none_p_kernel(tc, x_words, x_scales, wa, gt, w1, off
         w1q = keep.tile([P, N], U32, name="w1q", align_bytes=64)
         w1c = keep.tile([P, N], U8, name="w1c", align_bytes=64)
 
-        ssum = [keep.tile([P, PACK, HALF], F32, name=f"ssum{u}") for u in range(2)]
-        da = [keep.tile([P, PACK, HALF], F32, name=f"da{u}") for u in range(2)]
-        db = [keep.tile([P, PACK, HALF], F32, name=f"db{u}") for u in range(2)]
-        zb = [keep.tile([P, HALF, PACK], BF16, name=f"zb{u}", align_bytes=64) for u in range(2)]
+        ssum = keep.tile([P, PACK, H], F32, name="ssum")
+        da = keep.tile([P, PACK, H], F32, name="da")
+        db = keep.tile([P, PACK, H], F32, name="db")
+        zb = keep.tile([P, H, PACK], BF16, name="zb", align_bytes=64)
         zq = keep.tile([P, H], U32, name="zq", align_bytes=64)
         zs = keep.tile([P, H], U8, name="zs", align_bytes=64)
-        hps = [psum.tile([P, H], F32, name=f"hps{t}") for t in range(PACK - 1)]
-        hps.append(psum.tile([P, H], F32, name="hps3", tag="bank00"))
+        chunks = [slice(0, 256), slice(256, 384), slice(384, 512)]
+        h0 = [psum.tile([P, c.stop - c.start], F32, name=f"h0{c.start}") for c in chunks]
+        hps = [None] + [psum.tile([P, H], F32, name=f"hps{t}", tag=f"bank{t}") for t in range(1, PACK)]
         hm = [keep.tile([P, H], F32, name=f"hm{t}") for t in range(PACK)]
+        whole = slice(0, H)
 
-        def g_sum(u, t):
-            nc.vector.tensor_tensor(ssum[u][:, t, :], ywin[t][:].indirect(n1_t[:, lhalves[u]]), ypl[t][:, halves[u]], ALU.add)
+        def fetch(dst, t, lst, cols, other, op):
+            lcols = slice(cols.start // 16, cols.stop // 16)
+            nc.vector.tensor_tensor(dst[:, cols], win[t][:].indirect(lst[:, lcols]), other[:, cols], op)
 
-        def g_diff(u, t):
-            nc.vector.tensor_tensor(da[u][:, t, :], ywin[t][:].indirect(n2_t[:, lhalves[u]]), ssum[u][:, t, :], ALU.subtract)
-            nc.vector.tensor_tensor(db[u][:, t, :], ywin[t][:].indirect(n3_t[:, lhalves[u]]), ssum[u][:, t, :], ALU.subtract)
+        def g_sum(t, cols):
+            fetch(ssum[:, t, :], t, n1_t, cols, ypl[t], ALU.add)
 
-        def z_max(u):
-            nc.vector.tensor_tensor(zb[u][:].rearrange("p (c i) j -> p c j i", i=2),
-                                    da[u][:].rearrange("p j (c i) -> p c j i", i=2),
-                                    db[u][:].rearrange("p j (c i) -> p c j i", i=2), ALU.max)
+        def g_diff(dst, lst, t, cols):
+            fetch(dst[:, t, :], t, lst, cols, ssum[:, t, :], ALU.subtract)
 
-        def z_quant(u):
-            nc.vector.quantize_mx(out=zq[:, halves[u]].bitcast(FP8X4), scales=zs[:, halves[u]], in_=zb[u][:].rearrange("p c j -> p (c j)"))
+        def z_max(cols):
+            nc.vector.tensor_tensor(zb[:, cols, :].rearrange("p (c i) j -> p c j i", i=2),
+                                    da[:, :, cols].rearrange("p j (c i) -> p c j i", i=2),
+                                    db[:, :, cols].rearrange("p j (c i) -> p c j i", i=2), ALU.max)
 
-        def h_half(u):
-            for t in range(PACK):
-                mm(hps[t][:, halves[u]], w1q, w1c, t, zq, zs, halves[u])
-            for t in range(PACK):
-                nc.scalar.activation(hwin[t][:, halves[u]], hps[t][:, halves[u]], COPY, scale=-1.0)
-                nc.scalar.activation(hm[t][:, halves[u]], hps[t][:, halves[u]], COPY, scale=0.75)
+        def quant(q, s, b, cols):
+            nc.vector.quantize_mx(out=q[:, cols].bitcast(FP8X4), scales=s[:, cols], in_=b[:, cols, :].rearrange("p c j -> p (c j)"))
 
-        steps = [(u, t) for u in range(2) for t in range(PACK)]
-        g_sum(*steps[0])
-        for i, (u, t) in enumerate(steps):
-            if i + 1 < len(steps):
-                g_sum(*steps[i + 1])
-            g_diff(u, t)
-            if i == PACK:
-                z_max(0)
-            if i == PACK + 1:
-                z_quant(0)
-                nc.vector.quantize_mx(out=w1q[:].bitcast(FP8X4), scales=w1c[:], in_=w1b[:].rearrange("p c j -> p (c j)"))
-                h_half(0)
-        z_max(1)
-        z_quant(1)
-        h_half(1)
+        for u in range(2):
+            g_sum(0, halves[u])
+        for u in range(2):
+            g_diff(da, n2_t, 0, halves[u])
+        for t in range(1, PACK):
+            g_sum(t, whole)
+            g_diff(db, n3_t, t - 1, whole)
+            g_diff(da, n2_t, t, whole)
+        quant(w1q, w1c, w1b, slice(0, P))
+        for u in range(2):
+            g_diff(db, n3_t, PACK - 1, halves[u])
+
+        z_max(chunks[0])
+        for c, cols in enumerate(chunks):
+            if c + 1 < len(chunks):
+                z_max(chunks[c + 1])
+            quant(zq, zs, zb, cols)
+            mm(h0[c][:], w1q, w1c, 0, zq, zs, cols)
+            nc.scalar.activation(win[0][:, cols], h0[c][:], COPY, scale=-1.0)
+            if c == 0:
+                nc.scalar.activation(hm[0][:, cols], h0[c][:], COPY, scale=0.75)
+        for c in (1, 2):
+            nc.scalar.activation(hm[0][:, chunks[c]], h0[c][:], COPY, scale=0.75)
+        for t in range(1, PACK):
+            quant(w1q, w1c, w1b, slice(t * P, (t + 1) * P))
+        for t in range(1, PACK):
+            mm(hps[t][:], w1q, w1c, t, zq, zs, whole)
+            nc.scalar.activation(win[t][:, whole], hps[t][:], COPY, scale=-1.0)
+            nc.scalar.activation(hm[t][:], hps[t][:], COPY, scale=0.75)
 
         out_v = out.rearrange("(p t) c -> p t c", t=PACK)
-        pieces = [(t, slice(0, H), slice(0, 2 * LCOLS)) for t in range(PACK - 1)]
-        pieces = pieces + [(PACK - 1, halves[u], lhalves[u]) for u in range(2)]
         ea = [keep.tile([P, H], F32, name=f"ea{t}") for t in range(PACK)]
         eb = [keep.tile([P, H], F32, name=f"eb{t}") for t in range(PACK)]
         res = [keep.tile([P, H], F32, name=f"res{t}") for t in range(PACK)]
 
-        def fetch(dst, lst, piece):
-            t, cols, lc = piece
-            nc.vector.tensor_tensor(dst[t][:, cols], hwin[t][:].indirect(lst[:, lc]), hm[t][:, cols], ALU.add)
-
-        fetch(ea, n4_t, pieces[0])
-        for i, piece in enumerate(pieces):
-            t, cols, lc = piece
-            fetch(eb, n5_t, piece)
-            if i + 1 < len(pieces):
-                fetch(ea, n4_t, pieces[i + 1])
+        def finish(t, cols):
             nc.vector.tensor_tensor(res[t][:, cols], ea[t][:, cols], eb[t][:, cols], ALU.max)
             nc.sync.dma_start(out_v[:, t, cols], res[t][:, cols])
+
+        for u in range(2):
+            fetch(ea[0], 0, n4_t, halves[u], hm[0], ALU.add)
+        for t in range(PACK - 1):
+            fetch(eb[t], t, n5_t, whole, hm[t], ALU.add)
+            fetch(ea[t + 1], t + 1, n4_t, whole, hm[t + 1], ALU.add)
+            finish(t, whole)
+        for u in range(2):
+            fetch(eb[PACK - 1], PACK - 1, n5_t, halves[u], hm[PACK - 1], ALU.add)
+        for u in range(2):
+            finish(PACK - 1, halves[u])

@@ -37,21 +37,18 @@ def tile_picked_toktrimover_none_p_kernel(tc, x_words, x_scales, wa, gt, w1, off
         xs = keep.tile([P, T], U8, name="xs", align_bytes=64)
         nc.vector.memset(xs[:].bitcast(I32), 0)
         offs_t = load_list(offs, "offs_t")
+        wa_raw = keep.tile([P, PACK, H], F32, name="wa_raw", tag="weights")
+        nc.sync.dma_start(wa_raw[:], wa.rearrange("(p j) c -> p j c", j=PACK))
+        xw = keep.tile([P, T], I32, name="xw", align_bytes=64)
+        nc.sync.dma_start(xw[:], x_words[0].rearrange("p n t -> p (n t)").bitcast(I32))
         gt_t = keep.tile([P, PACK], F32, name="gt_t")
         nc.sync.dma_start(gt_t[:], gt.rearrange("(p j) o -> p (j o)", j=PACK))
         n1_t = load_list(n1, "n1_t")
         n2_t = load_list(n2, "n2_t")
-        wa_raw = keep.tile([P, PACK, H], F32, name="wa_raw")
-        nc.sync.dma_start(wa_raw[:], wa.rearrange("(p j) c -> p j c", j=PACK))
-        xw = keep.tile([P, T], I32, name="xw", align_bytes=64)
-        nc.sync.dma_start(xw[:], x_words[0].rearrange("p n t -> p (n t)").bitcast(I32))
         n3_t = load_list(n3, "n3_t")
+        nc.scalar.dma_start(xs[0:P:8, :].bitcast(I32), x_scales[0].bitcast(I32))
         n4_t = load_list(n4, "n4_t")
-        for q in range(4):
-            nc.scalar.dma_start(xs[32 * q : 32 * q + 4, :].bitcast(I32), x_scales[0][4 * q : 4 * q + 4, :].bitcast(I32))
         n5_t = load_list(n5, "n5_t")
-        w1_raw = keep.tile([P, PACK, N], F32, name="w1_raw")
-        nc.sync.dma_start(w1_raw[:], w1.rearrange("(p j) c -> p j c", j=PACK))
 
         win = [keep.tile([P, 2 * H], F32, name=f"win{t}") for t in range(PACK)]
         for t in range(PACK):
@@ -79,9 +76,13 @@ def tile_picked_toktrimover_none_p_kernel(tc, x_words, x_scales, wa, gt, w1, off
         weave(nc.scalar.copy, 1)
         gb = keep.tile([P, S], U8, name="gb", align_bytes=64)
         nc.vector.tensor_copy(gb[:], xs[:].indirect(offs_t[:]))
-        weave(nc.vector.tensor_copy, 2)
+        gbs = keep.tile([P, S], U8, name="gbs", align_bytes=64)
+        nc.vector.tensor_copy(gbs[:].rearrange("p (t m) -> p t m", t=PACK), gb[:].rearrange("p (m t) -> p t m", t=PACK))
         gbd = keep.tile([P, S], U8, name="gbd", align_bytes=64)
-        nc.vector.tensor_copy(gbd[:].rearrange("p (t m) -> p t m", t=PACK), gb[:].rearrange("p (m t) -> p t m", t=PACK))
+        nc.vector.memset(gbd[:].bitcast(I32), 0)
+        for q in range(4):
+            nc.sync.dma_start(gbd[32 * q : 32 * q + 4, :].bitcast(I32), gbs[32 * q : 32 * q + 32 : 8, :].bitcast(I32))
+        weave(nc.vector.tensor_copy, 2)
         wa_quant(2)
         wa_quant(0)
         wa_quant(1)
@@ -109,6 +110,8 @@ def tile_picked_toktrimover_none_p_kernel(tc, x_words, x_scales, wa, gt, w1, off
             nc.scalar.activation(win[t][:, :H], yps[t][:], COPY, scale=mag[:, t : t + 1])
             nc.scalar.activation(ypl[t][:], yps[t][:], COPY, scale=mag[:, t : t + 1])
 
+        w1_raw = keep.tile([P, PACK, N], F32, name="w1_raw", tag="weights")
+        nc.sync.dma_start(w1_raw[:], w1.rearrange("(p j) c -> p j c", j=PACK))
         w1s = keep.tile([P, PACK, N], BF16, name="w1s")
         for j in range(PACK):
             nc.scalar.activation(w1s[:, j, :], w1_raw[:, j, :], COPY, scale=sgn[:, j : j + 1])

from contextlib import ExitStack

import concourse.mybir as mybir

K, T, S, N, H = 512, 2048, 512, 512, 512
FLOPS = 2 * K * S * H + 2 * S * N * H

F32 = mybir.dt.float32
BF16 = mybir.dt.bfloat16
I32 = mybir.dt.int32
U32 = mybir.dt.uint32
U16 = mybir.dt.uint16
U8 = mybir.dt.uint8
FP8X4 = mybir.dt.float8_e4m3fn_x4
ALU = mybir.AluOpType
COPY = mybir.ActivationFunctionType.Copy

P = 128
PACK = 4
HALF = H // 2
LCOLS = HALF // 16


def tile_picked_toktrimover_none_p_kernel(tc, x_words, x_scales, wa, gt, w1, offs, n1, n2, n3, n4, n5, out):
    nc = tc.nc
    halves = [slice(0, HALF), slice(HALF, H)]
    lhalves = [slice(0, LCOLS), slice(LCOLS, 2 * LCOLS)]
    with ExitStack() as ctx:
        keep = ctx.enter_context(tc.tile_pool(name="keep", bufs=1))
        psum = ctx.enter_context(tc.psum_pool(name="psum", bufs=1))

        def load_list(src, name):
            tile = keep.tile([P, S // 16], U16, name=name)
            nc.sync.dma_start(tile[:], src)
            return tile

        xs = keep.tile([P, T], U8, name="xs", align_bytes=64)
        nc.vector.memset(xs[:].bitcast(I32), 0)
        offs_t = load_list(offs, "offs_t")
        wa_raw = keep.tile([P, PACK, H], F32, name="wa_raw", tag="weights")
        nc.sync.dma_start(wa_raw[:], wa.rearrange("(p j) c -> p j c", j=PACK))
        xw = keep.tile([P, T], I32, name="xw", align_bytes=64)
        nc.sync.dma_start(xw[:], x_words[0].rearrange("p n t -> p (n t)").bitcast(I32))
        gt_t = keep.tile([P, PACK], F32, name="gt_t")
        nc.sync.dma_start(gt_t[:], gt.rearrange("(p j) o -> p (j o)", j=PACK))
        n1_t = load_list(n1, "n1_t")
        n2_t = load_list(n2, "n2_t")
        n3_t = load_list(n3, "n3_t")
        nc.scalar.dma_start(xs[0:P:8, :].bitcast(I32), x_scales[0].bitcast(I32))
        n4_t = load_list(n4, "n4_t")
        n5_t = load_list(n5, "n5_t")

        win = [keep.tile([P, 2 * H], F32, name=f"win{t}") for t in range(PACK)]
        for t in range(PACK):
            nc.vector.memset(win[t][:, H:], 0.0)

        sgn2 = keep.tile([P, PACK], F32, name="sgn2")
        sgn = keep.tile([P, PACK], F32, name="sgn")
        mag = keep.tile([P, PACK], F32, name="mag")
        nc.gpsimd.tensor_scalar(sgn2[:], gt_t[:], 0.0, 2.0, ALU.is_ge, ALU.mult)
        nc.gpsimd.tensor_scalar(sgn[:], sgn2[:], 1.0, -1.0, ALU.mult, ALU.add)
        nc.gpsimd.tensor_tensor(mag[:], gt_t[:], sgn[:], ALU.mult)

        waq = keep.tile([P, H], U32, name="waq", align_bytes=64)
        was = keep.tile([P, H], U8, name="was", align_bytes=64)
        wa_cuts = [slice(0, 256), slice(256, 384), slice(384, 512)]
        wab = [keep.tile([P, c.stop - c.start, PACK], BF16, name=f"wab{c.start}", align_bytes=64) for c in wa_cuts]

        def weave(copy, c):
            copy(wab[c][:].rearrange("p (c i) j -> p c j i", i=2), wa_raw[:, :, wa_cuts[c]].rearrange("p j (c i) -> p c j i", i=2))

        def wa_quant(c):
            nc.vector.quantize_mx(out=waq[:, wa_cuts[c]].bitcast(FP8X4), scales=was[:, wa_cuts[c]], in_=wab[c][:].rearrange("p c j -> p (c j)"))

        weave(nc.scalar.copy, 0)
        weave(nc.scalar.copy, 1)
        gb = keep.tile([P, S], U8, name="gb", align_bytes=64)
        nc.vector.tensor_copy(gb[:], xs[:].indirect(offs_t[:]))
        gbs = keep.tile([P, S], U8, name="gbs", align_bytes=64)
        nc.vector.tensor_copy(gbs[:].rearrange("p (t m) -> p t m", t=PACK), gb[:].rearrange("p (m t) -> p t m", t=PACK))
        gbd = keep.tile([P, S], U8, name="gbd", align_bytes=64)
        nc.vector.memset(gbd[:].bitcast(I32), 0)
        for q in range(4):
            nc.sync.dma_start(gbd[32 * q : 32 * q + 4, :].bitcast(I32), gbs[32 * q : 32 * q + 32 : 8, :].bitcast(I32))
        weave(nc.vector.tensor_copy, 2)
        wa_quant(2)
        wa_quant(0)
        wa_quant(1)
        gw = keep.tile([P, S], U32, name="gw", align_bytes=64)
        nc.vector.tensor_copy(gw[:].rearrange("p (t m) -> p m t", t=PACK), xw[:].bitcast(U32).indirect(offs_t[:]))

        def mm(dst, lq, ls, t, rq, rs, cols):
            tcols = slice(t * P, (t + 1) * P)
            nc.tensor.matmul_mx(out=dst, lhsT=lq[:, tcols].bitcast(FP8X4), lhsT_scale=ls[:, tcols],
                                rhs=rq[:, cols].bitcast(FP8X4), rhs_scale=rs[:, cols], start=True, stop=True)

        ypl = [keep.tile([P, H], F32, name=f"ypl{t}") for t in range(PACK)]
        y0 = [psum.tile([P, HALF], F32, name=f"y0{u}", tag=f"bank0{u}") for u in range(2)]
        for u in range(2):
            mm(y0[u][:], gw, gbd, 0, waq, was, halves[u])
        yps = [None] + [psum.tile([P, H], F32, name=f"yps{t}", tag=f"bank{t}") for t in range(1, PACK)]
        for t in range(1, PACK):
            mm(yps[t][:], gw, gbd, t, waq, was, slice(0, H))

        nc.scalar.activation(win[0][:, halves[0]], y0[0][:], COPY, scale=mag[:, 0:1])
        nc.vector.tensor_scalar(win[0][:, halves[1]], y0[1][:], mag[:, 0:1], None, ALU.mult)
        nc.scalar.activation(ypl[0][:, halves[0]], y0[0][:], COPY, scale=mag[:, 0:1])
        nc.scalar.activation(ypl[0][:, halves[1]], y0[1][:], COPY, scale=mag[:, 0:1])
        for t in range(1, PACK):
            nc.scalar.activation(win[t][:, :H], yps[t][:], COPY, scale=mag[:, t : t + 1])
            nc.scalar.activation(ypl[t][:], yps[t][:], COPY, scale=mag[:, t : t + 1])

        w1_raw = keep.tile([P, PACK, N], F32, name="w1_raw", tag="weights")
        nc.sync.dma_start(w1_raw[:], w1.rearrange("(p j) c -> p j c", j=PACK))
        w1s = keep.tile([P, PACK, N], BF16, name="w1s")
        for j in range(PACK):
            nc.scalar.activation(w1s[:, j, :], w1_raw[:, j, :], COPY, scale=sgn[:, j : j + 1])
        w1b = keep.tile([P, N, PACK], BF16, name="w1b", align_bytes=64)
        for t in range(PACK):
            nc.scalar.copy(w1b[:, t * P : (t + 1) * P, :], w1s[:].rearrange("p j (m t) -> p t m j", t=PACK)[:, t])
        w1q = keep.tile([P, N], U32, name="w1q", align_bytes=64)
        w1c = keep.tile([P, N], U8, name="w1c", align_bytes=64)

        ssum = keep.tile([P, PACK, H], F32, name="ssum")
        da = keep.tile([P, PACK, H], F32, name="da")
        db = keep.tile([P, PACK, H], F32, name="db")
        zb = keep.tile([P, H, PACK], BF16, name="zb", align_bytes=64)
        zq = keep.tile([P, H], U32, name="zq", align_bytes=64)
        zs = keep.tile([P, H], U8, name="zs", align_bytes=64)
        chunks = [slice(0, 256), slice(256, 384), slice(384, 512)]
        h0 = [psum.tile([P, c.stop - c.start], F32, name=f"h0{c.start}") for c in chunks]
        hps = [None] + [psum.tile([P, H], F32, name=f"hps{t}", tag=f"bank{t}") for t in range(1, PACK)]
        hm = [keep.tile([P, H], F32, name=f"hm{t}") for t in range(PACK)]
        whole = slice(0, H)

        def fetch(dst, t, lst, cols, other, op):
            lcols = slice(cols.start // 16, cols.stop // 16)
            nc.vector.tensor_tensor(dst[:, cols], win[t][:].indirect(lst[:, lcols]), other[:, cols], op)

        def g_sum(t, cols):
            fetch(ssum[:, t, :], t, n1_t, cols, ypl[t], ALU.add)

        def g_diff(dst, lst, t, cols):
            fetch(dst[:, t, :], t, lst, cols, ssum[:, t, :], ALU.subtract)

        def z_max(cols):
            nc.vector.tensor_tensor(zb[:, cols, :].rearrange("p (c i) j -> p c j i", i=2),
                                    da[:, :, cols].rearrange("p j (c i) -> p c j i", i=2),
                                    db[:, :, cols].rearrange("p j (c i) -> p c j i", i=2), ALU.max)

        def quant(q, s, b, cols):
            nc.vector.quantize_mx(out=q[:, cols].bitcast(FP8X4), scales=s[:, cols], in_=b[:, cols, :].rearrange("p c j -> p (c j)"))

        for u in range(2):
            g_sum(0, halves[u])
        for u in range(2):
            g_diff(da, n2_t, 0, halves[u])
        for t in range(1, PACK):
            g_sum(t, whole)
            g_diff(db, n3_t, t - 1, whole)
            g_diff(da, n2_t, t, whole)
        quant(w1q, w1c, w1b, slice(0, P))
        for u in range(2):
            g_diff(db, n3_t, PACK - 1, halves[u])

        z_max(chunks[0])
        for c, cols in enumerate(chunks):
            if c + 1 < len(chunks):
                z_max(chunks[c + 1])
            quant(zq, zs, zb, cols)
            mm(h0[c][:], w1q, w1c, 0, zq, zs, cols)
            nc.scalar.activation(win[0][:, cols], h0[c][:], COPY, scale=-1.0)
            if c == 0:
                nc.scalar.activation(hm[0][:, cols], h0[c][:], COPY, scale=0.75)
        for c in (1, 2):
            nc.scalar.activation(hm[0][:, chunks[c]], h0[c][:], COPY, scale=0.75)
        for t in range(1, PACK):
            quant(w1q, w1c, w1b, slice(t * P, (t + 1) * P))
        for t in range(1, PACK):
            mm(hps[t][:], w1q, w1c, t, zq, zs, whole)
            nc.scalar.activation(win[t][:, whole], hps[t][:], COPY, scale=-1.0)
            nc.scalar.activation(hm[t][:], hps[t][:], COPY, scale=0.75)

        out_v = out.rearrange("(p t) c -> p t c", t=PACK)
        ea = [keep.tile([P, H], F32, name=f"ea{t}") for t in range(PACK)]
        eb = [keep.tile([P, H], F32, name=f"eb{t}") for t in range(PACK)]
        res = [keep.tile([P, H], F32, name=f"res{t}") for t in range(PACK)]

        def finish(t, cols):
            nc.vector.tensor_tensor(res[t][:, cols], ea[t][:, cols], eb[t][:, cols], ALU.max)
            nc.sync.dma_start(out_v[:, t, cols], res[t][:, cols])

        for u in range(2):
            fetch(ea[0], 0, n4_t, halves[u], hm[0], ALU.add)
        for t in range(PACK - 1):
            fetch(eb[t], t, n5_t, whole, hm[t], ALU.add)
            fetch(ea[t + 1], t + 1, n4_t, whole, hm[t + 1], ALU.add)
            finish(t, whole)
        for u in range(2):
            fetch(eb[PACK - 1], PACK - 1, n5_t, halves[u], hm[PACK - 1], ALU.add)
        for u in range(2):
            finish(PACK - 1, halves[u])
